import numpy as np, ml_dtypes
CORES = [34,162,290,418,42,426]
N = 6
TK = 64
def setup_inputs(rng):
    return {"x": rng.standard_normal((N, 128, TK), dtype=np.float32).astype(ml_dtypes.bfloat16), "w": rng.standard_normal((N, 128, 128), dtype=np.float32).astype(ml_dtypes.bfloat16)}
def setup_inputs_big(rng):
    d = setup_inputs(rng)
    for k in ("x", "w"): d[k] = (d[k].astype(np.float32) * 1024.0).astype(d[k].dtype)
    return d
def setup_inputs_small(rng):
    d = setup_inputs(rng)
    for k in ("x", "w"): d[k] = (d[k].astype(np.float32) * (1 / 1024.0)).astype(d[k].dtype)
    return d
def setup_inputs_apart(rng):
    d = setup_inputs(rng)
    f = (10.0 ** rng.permutation(np.linspace(-1.5, 1.5, N))).astype(np.float32).reshape(N, 1, 1)
    for k in ("x", "w"): d[k] = (d[k].astype(np.float32) * f).astype(d[k].dtype)
    return d
def setup_inputs_neg(rng):
    d = setup_inputs(rng)
    d["x"] = (np.abs(d["x"].astype(np.float32)) * 1048576.0).astype(d["x"].dtype); d["w"] = (-np.abs(d["w"].astype(np.float32))).astype(d["w"].dtype)
    return d
def reference(x, w):
    X, W = x.astype(np.float64), w.astype(np.float64)
    y = np.stack([np.max([W[j].T @ X[r] for j in range(N)], axis=0) for r in range(N)])
    return {"y": y.astype(ml_dtypes.bfloat16)}

from concourse.bass import DstId, RemoteDMATransfer
from concourse.mybir import AluOpType

TK = 64
M = 128
G = 3

SCRATCH = {
    "xx": ("sbuf", [128, 2 * TK], "bfloat16"),
    "ww": ("sbuf", [128, G * M], "bfloat16"),
    "res": ("sbuf", [128, TK], "bfloat16"),
    "got": ("sbuf", [128, TK], "bfloat16"),
    "ysb": ("sbuf", [128, TK], "bfloat16"),
    "tp1": ("sbuf", [128, TK], "float32"),
    "tp2": ("sbuf", [128, TK], "float32"),
    "to1": ("sbuf", [128, TK], "float32"),
    "to2": ("sbuf", [128, TK], "float32"),
    "p0": ("psum", [128, 512], "float32"),
    "p1": ("psum", [128, 512], "float32"),
    "p2": ("psum", [128, 512], "float32"),
    "po": ("psum", [128, 512], "float32"),
}
SEMAPHORES = ["lx", "lw", "ax", "aw0", "aw1", "aw2", "ar", "sent",
              "mp0", "mp1", "mp2", "mo", "v", "vres", "vfin", "st"]


def _count(mask):
    return bin(mask).count("1")


def rank_program(g, core, T, topo):
    if T.rank_of(core) is None:
        return
    S = T.sem
    my_rack = topo.rack(topo.host(core))
    group = [q for q in T.cores if topo.rack(topo.host(q)) == my_rack]
    me = group.index(core)
    partner = [q for q in T.cores
               if topo.rack(topo.host(q)) != my_rack and topo.chip(q) == topo.chip(core)
               and topo.may_write(core, q) and topo.may_write(q, core)][0]
    others = [group[(me + k) % G] for k in range(1, G)]
    arrival = [me] + [(me - k) % G for k in range(1, G)]

    def wslot(i):
        return T.ww[:, i * M:(i + 1) * M]

    x_own, x_far = T.xx[:, 0:TK], T.xx[:, TK:2 * TK]
    p_rid, p_pid = topo.addr(partner, core)
    p_mask = topo.mask(core, partner)
    w_mask = p_mask
    for d in others:
        w_mask &= topo.mask(core, d)

    g.sync.dma_start(x_own, T.x[:]).then_inc(S.lx, 16)
    g.scalar.dma_start(wslot(me), T.w[:]).then_inc(S.lw, 16)

    g.wait_ge(S.lx, 16)
    g.remote_dma(out_ap=x_far, in_ap=x_own, remote_sem=S.ax, local_sem=S.sent,
                 pid=p_pid, routing_id=p_rid, dma_engine_mask=p_mask)
    g.wait_ge(S.lw, 16)
    ids = []
    for d in others:
        rid, pid = topo.addr(d, core)
        ids.append(DstId(rid=rid, pnc=pid))
    g.remote_dma_fused([RemoteDMATransfer(dst_ids=ids, dma_engine_mask=w_mask, remote_sem=S["aw%d" % me],
                                          srcs=[wslot(me)], dsts=[wslot(me) for _ in others])],
                       local_sem=S.sent)
    g.wait_ge(S.vres, 1)
    g.remote_dma(out_ap=T.got[:], in_ap=T.res[:], remote_sem=S.ar, local_sem=S.sent,
                 pid=p_pid, routing_id=p_rid, dma_engine_mask=p_mask)
    g.wait_ge(S.sent, 2 * _count(p_mask) + _count(w_mask))

    t = g.tensor
    t.wait_ge(S.lw, 16)
    t.wait_ge(S.ax, _count(p_mask))
    for n, i in enumerate(arrival):
        if n:
            t.wait_ge(S["aw%d" % i], _count(w_mask))
        t.matmul(T["p%d" % n][:, 0:TK], wslot(i), x_far, True, True).then_inc(S["mp%d" % n], 1)
    t.wait_ge(S.lx, 16)
    for n, i in enumerate(arrival):
        t.matmul(T.po[:, n * TK:(n + 1) * TK], wslot(i), x_own, True, True).then_inc(S.mo, 1)

    v = g.vector
    mx = AluOpType.max
    v.wait_ge(S.mp0, 1)
    v.tensor_copy(T.tp1[:], T.p0[:, 0:TK]).then_inc(S.v, 1)
    v.wait_ge(S.mp1, 1)
    v.wait_ge(S.v, 1)
    v.tensor_tensor(T.tp2[:], T.tp1[:], T.p1[:, 0:TK], mx).then_inc(S.v, 1)
    v.wait_ge(S.mp2, 1)
    v.wait_ge(S.v, 2)
    v.tensor_tensor(T.res[:], T.tp2[:], T.p2[:, 0:TK], mx).then_inc(S.vres, 1)
    v.wait_ge(S.mo, G)
    v.tensor_copy(T.to1[:], T.po[:, 0:TK]).then_inc(S.v, 1)
    v.wait_ge(S.v, 3)
    v.tensor_tensor(T.to2[:], T.to1[:], T.po[:, TK:2 * TK], mx).then_inc(S.v, 1)
    v.wait_ge(S.v, 4)
    v.tensor_tensor(T.po[:, 3 * TK:4 * TK], T.to2[:], T.po[:, 2 * TK:3 * TK], mx).then_inc(S.v, 1)
    v.wait_ge(S.v, 5)
    v.wait_ge(S.ar, _count(p_mask))
    v.tensor_tensor(T.ysb[:], T.po[:, 3 * TK:4 * TK], T.got[:], mx).then_inc(S.vfin, 1)

    g.sync.wait_ge(S.vfin, 1)
    g.sync.dma_start(T.y[:], T.ysb[:]).then_inc(S.st, 16)
    g.sync.wait_ge(S.st, 16)
